import numpy as np
import ml_dtypes


def mxq(x, axis, fmt="e4m3"):
    dtype, down = {"e4m3": (ml_dtypes.float8_e4m3fn, 7), "e5m2": (ml_dtypes.float8_e5m2, 14)}[fmt]
    v = np.moveaxis(np.asarray(x, np.float32).astype(ml_dtypes.bfloat16).astype(np.float64), axis, -1)
    blocks = v.reshape(v.shape[:-1] + (-1, 32))
    amax = np.abs(blocks).max(-1, keepdims=True)
    byte = np.maximum(np.where(amax > 0, np.frexp(amax)[1] - 1 + 127, 0) - down, 1)
    scale = np.exp2(byte - 127.0)
    codes = (blocks / scale).astype(np.float32).astype(dtype).astype(np.float64)
    return np.moveaxis((codes * scale).reshape(v.shape), -1, axis)


WIDE = False


def mx_kscale(k):
    if not WIDE:
        return np.ones(k)
    levels = np.array([10, -10, 5, -5, 0])
    if k % 512:
        return np.exp2(np.random.permutation(np.resize(levels, k // 32))).repeat(32)
    a = np.empty((k // 512, 16))
    for p in range(k // 512):
        a[p, :8] = np.random.permutation(np.resize(levels, 8))
        for g in range(8):
            far = levels[np.abs(levels - a[p, g]) >= 10]
            a[p, g + 8] = far[np.random.randint(len(far))]
    return np.exp2(a.ravel()).repeat(32)


def f64(x):
    return np.asarray(x).astype(np.float64)


def striped(idx):
    return np.tile(idx.reshape(-1, 16).T, (8, 1)).astype(np.uint16)


def unstriped(offs):
    return offs[:16].T.reshape(-1).astype(np.int64)


def pack_weight(w):
    k, n = w.shape
    w = f64(np.asarray(w, np.float32).astype(ml_dtypes.bfloat16)).reshape(k // 32, 32, n)
    amax = np.abs(w).max(1)
    byte = np.clip(np.where(amax > 0, np.frexp(amax)[1] - 1 + 127 - 7, 1), 1, 254)
    scaled = (w * np.exp2(127.0 - byte)[:, None, :]).reshape(k, n).astype(np.float32)
    words = np.ascontiguousarray(scaled.reshape(k // 512, 128, 4, n).transpose(0, 1, 3, 2)).astype(ml_dtypes.float8_e4m3fn).view(np.uint8)
    return words, np.ascontiguousarray(byte.astype(np.uint8).reshape(k // 512, 16, n))


def unpack_weight(words, scales):
    g, p, n, _ = words.shape
    vals = np.ascontiguousarray(words).view(ml_dtypes.float8_e4m3fn).astype(np.float64) * np.repeat(np.exp2(scales.astype(np.float64) - 127.0), 8, axis=1)[..., None]
    return vals.transpose(0, 1, 3, 2).reshape(g * 512, n)


def sigmoid(v):
    return 1.0 / (1.0 + np.exp(-np.maximum(v, -700.0)))


def silu(v):
    return v / (1.0 + np.exp(-np.maximum(v, -700.0)))


K, T, S, N, H, V = 512, 1024, 512, 128, 512, 256


def setup_inputs():
    n = np.random.standard_normal
    s = mx_kscale(K)[:, None]
    u = mx_kscale(H)
    packed_xT = pack_weight(n((K, T)) * s)
    return {
        "x_words": packed_xT[0],
        "x_scales": packed_xT[1],
        "w1": (n((K, H)) / np.sqrt(K) / s).astype(np.float32),
        "w2": (n((K, H)) / np.sqrt(K) / s).astype(np.float32),
        "ctx2": (n((H, V))).astype(np.float32),
        "gn": (np.random.uniform(0.5, 1.5, (H, S))).astype(np.float32),
        "unit": (np.random.uniform(0.6, 1.4, (H, 1)) * u[:, None]).astype(np.float32),
        "w3": (n((H, N)) / np.sqrt(H) / u[:, None]).astype(np.float32),
        "offs": striped(np.random.permutation(T)[:S]),
        "sel": striped(np.random.permutation(S)[:V]),
    }


def reference(x_words, x_scales, w1, w2, ctx2, gn, unit, w3, offs, sel):
    xq = unpack_weight(x_words, x_scales)[:, unstriped(offs)]
    yr = mxq(f64(w2), 0, "e4m3").T @ xq
    rs = yr[:, unstriped(sel)]
    rw = sigmoid(rs)
    y = mxq(f64(w1), 0, "e4m3").T @ xq
    xs = y[:, unstriped(sel)]
    upd = rw * (silu(xs + f64(ctx2)))
    merged = y.copy()
    merged[:, unstriped(sel)] = upd
    mg2 = merged * f64(gn)
    hid = f64(unit) * mg2
    return mxq(f64(w3), 0, "e4m3").T @ mxq(hid, 0, "e4m3")

@@ -1,0 +1,199 @@
+from contextlib import ExitStack
+
+import concourse.mybir as mybir
+
+K, T, S, N, H, V = 512, 1024, 512, 128, 512, 256
+FLOPS = 2 * K * H * S * 2 + 2 * H * N * S
+
+F32 = mybir.dt.float32
+BF16 = mybir.dt.bfloat16
+I32 = mybir.dt.int32
+U32 = mybir.dt.uint32
+U16 = mybir.dt.uint16
+U8 = mybir.dt.uint8
+FP8X4 = mybir.dt.float8_e4m3fn_x4
+ACT = mybir.ActivationFunctionType
+ALU = mybir.AluOpType
+
+P = 128
+PACK = 4
+HALF = H // 2
+SCATTER_ON_VECTOR = (0, 3)
+
+
+def tile_picked_ymodsk_gain_p_kernel(
+    tc, x_words, x_scales, w1, w2, ctx2, gn, unit, w3, offs, sel, out
+):
+    nc = tc.nc
+    with ExitStack() as ctx:
+        keep = ctx.enter_context(tc.tile_pool(name="keep", bufs=1))
+        psum = ctx.enter_context(tc.psum_pool(name="psum", bufs=1))
+
+        offs_sb = keep.tile([P, S // 16], U16, name="offs_sb")
+        sel_sb = keep.tile([P, V // 16], U16, name="sel_sb")
+        table_words = keep.tile([P, T], U32, name="table_words", align_bytes=64)
+        table_bytes = keep.tile([P, T], U8, name="table_bytes", align_bytes=64)
+
+        nc.vector.memset(table_bytes[:].bitcast(I32), 0)
+        nc.sync.dma_start(offs_sb[:], offs)
+        nc.sync.dma_start(sel_sb[:], sel)
+        nc.sync.dma_start(
+            table_words[:].bitcast(I32), x_words[0].rearrange("p c r -> p (c r)").bitcast(I32)
+        )
+        for q in range(4):
+            nc.sync.dma_start(
+                table_bytes[32 * q : 32 * q + 4, :].bitcast(I32),
+                x_scales[0, 4 * q : 4 * q + 4, :].bitcast(I32),
+            )
+
+        def load_halves(w, name):
+            halves = []
+            for h in range(2):
+                raw = keep.tile([P, PACK, HALF], F32, name=f"{name}_raw{h}")
+                nc.sync.dma_start(
+                    raw[:], w.rearrange("(p j) c -> p j c", j=PACK)[:, :, h * HALF : (h + 1) * HALF]
+                )
+                halves.append(raw)
+            return halves
+
+        w2_raw = load_halves(w2, "w2")
+        w1_raw = load_halves(w1, "w1")
+        ctx_sb = keep.tile([P, PACK, V], F32, name="ctx_sb")
+        nc.sync.dma_start(ctx_sb[:], ctx2.rearrange("(p t) v -> p t v", t=PACK))
+        w3_raw = keep.tile([P, PACK, N], F32, name="w3_raw")
+        nc.sync.dma_start(w3_raw[:], w3.rearrange("(p j) c -> p j c", j=PACK))
+        unit_sb = keep.tile([P, PACK], F32, name="unit_sb")
+        nc.sync.dma_start(unit_sb[:], unit.rearrange("(p t) o -> p (t o)", t=PACK))
+        gn_sb = keep.tile([P, PACK, S], F32, name="gn_sb")
+        nc.sync.dma_start(gn_sb[:], gn.rearrange("(p t) c -> p t c", t=PACK))
+
+        x_codes = keep.tile([P, S], U32, name="x_codes", align_bytes=64)
+        x_plane = keep.tile([P, S], U8, name="x_plane", align_bytes=64)
+        nc.vector.tensor_copy(x_codes[:], table_words[:].indirect(offs_sb[:]))
+        nc.vector.tensor_copy(x_plane[:], table_bytes[:].indirect(offs_sb[:]))
+
+        def first_product(raw, name, first_half_copy):
+            grouped = keep.tile(
+                [P, PACK, P, PACK], BF16, name=f"{name}_grouped", tag=f"{name}_stage", align_bytes=64
+            )
+            for h, copy in enumerate((first_half_copy, nc.vector.tensor_copy)):
+                m_range = slice(h * P // 2, (h + 1) * P // 2)
+                copy(
+                    grouped[:, :, m_range, :].rearrange("p t m j -> p m j t"),
+                    raw[h][:].rearrange("p j (m t) -> p m j t", t=PACK),
+                )
+            banks = []
+            for t in range(PACK):
+                codes = keep.tile([P, P], U32, name=f"{name}_codes{t}", align_bytes=64)
+                plane = keep.tile([P, P], U8, name=f"{name}_plane{t}", align_bytes=64)
+                nc.vector.quantize_mx(
+                    out=codes[:].bitcast(FP8X4),
+                    scales=plane[:],
+                    in_=grouped[:, t, :, :].rearrange("p m j -> p (m j)"),
+                )
+                bank = psum.tile([P, S], F32, name=f"{name}_bank{t}")
+                nc.tensor.matmul_mx(
+                    out=bank[:],
+                    lhsT=codes[:].bitcast(FP8X4),
+                    lhsT_scale=plane[:],
+                    rhs=x_codes[:].bitcast(FP8X4),
+                    rhs_scale=x_plane[:],
+                    start=True,
+                    stop=True,
+                )
+                banks.append(bank)
+            return banks
+
+        score_banks = first_product(w2_raw, "w2", nc.scalar.copy)
+        half_tanhs = []
+        for t in range(PACK):
+            half_tanh = keep.tile([P, S], F32, name=f"half_tanh{t}")
+            nc.scalar.activation(half_tanh[:], score_banks[t][:], ACT.Tanh, scale=0.5)
+            half_tanhs.append(half_tanh)
+
+        value_banks = first_product(w1_raw, "w1", nc.vector.tensor_copy)
+        merged, pres = [], []
+        for t in range(PACK):
+            y = keep.tile([P, S], F32, name=f"merged{t}")
+            copy = nc.vector.tensor_copy if t == 0 else nc.scalar.copy
+            copy(y[:], value_banks[t][:])
+            pre = keep.tile([P, V], F32, name=f"pre{t}")
+            nc.vector.tensor_tensor(pre[:], y[:].indirect(sel_sb[:]), ctx_sb[:, t, :], ALU.add)
+            merged.append(y)
+            pres.append(pre)
+
+        w3_grouped = keep.tile([P, N, PACK], BF16, name="w3_grouped", align_bytes=64)
+        nc.vector.tensor_copy(
+            w3_grouped[:].rearrange("p (c i) j -> p c j i", i=4),
+            w3_raw[:].rearrange("p j (c i) -> p c j i", i=4),
+        )
+        w3_codes = keep.tile([P, N], U32, name="w3_codes", align_bytes=64)
+        w3_plane = keep.tile([P, N], U8, name="w3_plane", align_bytes=64)
+        nc.vector.quantize_mx(
+            out=w3_codes[:].bitcast(FP8X4),
+            scales=w3_plane[:],
+            in_=w3_grouped[:].rearrange("p c j -> p (c j)"),
+        )
+
+        gates, silus = [], []
+        gate_tile = keep.tile([P, PACK, V], F32, name="gate_tile", tag="w1_stage", align_bytes=64)
+        for t in range(PACK):
+            silu = keep.tile([P, V], F32, name=f"silu{t}")
+            nc.scalar.activation(silu[:], pres[t][:], ACT.Silu)
+            gate = gate_tile[:, t, :]
+            nc.scalar.activation(
+                gate, half_tanhs[t][:].indirect(sel_sb[:]), ACT.Copy, scale=0.5, bias=0.5
+            )
+            gates.append(gate)
+            silus.append(silu)
+
+        for t in range(PACK):
+            window = merged[t][:].indirect(sel_sb[:])
+            if t in SCATTER_ON_VECTOR:
+                nc.vector.tensor_tensor(window, gates[t], silus[t][:], ALU.mult)
+            else:
+                upd = keep.tile([P, V], F32, name=f"upd{t}")
+                nc.vector.tensor_tensor(upd[:], gates[t], silus[t][:], ALU.mult)
+                nc.scalar.activation(window, upd[:], ACT.Copy)
+
+        hid = [keep.tile([P, PACK, HALF], BF16, name=f"hid{h}") for h in range(2)]
+        for t in (0, 3, 1, 2):
+            for h in (1, 0):
+                cols = slice(h * HALF, (h + 1) * HALF)
+                nc.vector.scalar_tensor_tensor(
+                    hid[h][:, t, :],
+                    merged[t][:, cols],
+                    unit_sb[:, t : t + 1],
+                    gn_sb[:, t, cols],
+                    ALU.mult,
+                    ALU.mult,
+                )
+
+        copies = (nc.vector.tensor_copy, nc.scalar.copy)
+        for h in range(2):
+            cols = slice(h * HALF, (h + 1) * HALF)
+            grouped = keep.tile([P, HALF, PACK], BF16, name=f"hid_grouped{h}", align_bytes=64)
+            copies[h](
+                grouped[:].rearrange("p (c i) t -> p c t i", i=4),
+                hid[h][:].rearrange("p t (c i) -> p c t i", i=4),
+            )
+            codes = keep.tile([P, HALF], U32, name=f"hid_codes{h}", align_bytes=64)
+            plane = keep.tile([P, HALF], U8, name=f"hid_plane{h}", align_bytes=64)
+            nc.vector.quantize_mx(
+                out=codes[:].bitcast(FP8X4),
+                scales=plane[:],
+                in_=grouped[:].rearrange("p c t -> p (c t)"),
+            )
+            bank = psum.tile([P, S], F32, name=f"w2_bank{h}")
+            nc.tensor.matmul_mx(
+                out=bank[:, 0:HALF],
+                lhsT=w3_codes[:].bitcast(FP8X4),
+                lhsT_scale=w3_plane[:],
+                rhs=codes[:].bitcast(FP8X4),
+                rhs_scale=plane[:],
+                start=True,
+                stop=True,
+            )
+            result = keep.tile([P, HALF], F32, name=f"result{h}")
+            copies[1 - h](result[:], bank[:, 0:HALF])
+            nc.sync.dma_start(out[:, cols], result[:])

@@ -35,8 +35,10 @@ def tile_picked_ymodsk_gain_p_kernel(
         table_bytes = keep.tile([P, T], U8, name="table_bytes", align_bytes=64)
 
         nc.vector.memset(table_bytes[:].bitcast(I32), 0)
+        warm = keep.tile([P, 2], F32, name="warm")
+        nc.gpsimd.memset(warm[:, 0:1], 0.0)
+        nc.scalar.activation(warm[:, 1:2], warm[:, 0:1], ACT.Silu)
         nc.sync.dma_start(offs_sb[:], offs)
-        nc.sync.dma_start(sel_sb[:], sel)
         nc.sync.dma_start(
             table_words[:].bitcast(I32), x_words[0].rearrange("p c r -> p (c r)").bitcast(I32)
         )
@@ -49,7 +51,7 @@ def tile_picked_ymodsk_gain_p_kernel(
         def load_halves(w, name):
             halves = []
             for h in range(2):
-                raw = keep.tile([P, PACK, HALF], F32, name=f"{name}_raw{h}")
+                raw = keep.tile([P, PACK, HALF], F32, name=f"{name}_raw{h}", align_bytes=64)
                 nc.sync.dma_start(
                     raw[:], w.rearrange("(p j) c -> p j c", j=PACK)[:, :, h * HALF : (h + 1) * HALF]
                 )
@@ -58,6 +60,7 @@ def tile_picked_ymodsk_gain_p_kernel(
 
         w2_raw = load_halves(w2, "w2")
         w1_raw = load_halves(w1, "w1")
+        nc.sync.dma_start(sel_sb[:], sel)
         ctx_sb = keep.tile([P, PACK, V], F32, name="ctx_sb")
         nc.sync.dma_start(ctx_sb[:], ctx2.rearrange("(p t) v -> p t v", t=PACK))
         w3_raw = keep.tile([P, PACK, N], F32, name="w3_raw")
@@ -72,55 +75,59 @@ def tile_picked_ymodsk_gain_p_kernel(
         nc.vector.tensor_copy(x_codes[:], table_words[:].indirect(offs_sb[:]))
         nc.vector.tensor_copy(x_plane[:], table_bytes[:].indirect(offs_sb[:]))
 
-        def first_product(raw, name, first_half_copy):
+        def group_weight(raw, name, first_half_copy):
             grouped = keep.tile(
                 [P, PACK, P, PACK], BF16, name=f"{name}_grouped", tag=f"{name}_stage", align_bytes=64
             )
             for h, copy in enumerate((first_half_copy, nc.vector.tensor_copy)):
-                m_range = slice(h * P // 2, (h + 1) * P // 2)
                 copy(
-                    grouped[:, :, m_range, :].rearrange("p t m j -> p m j t"),
+                    grouped[:, :, h * P // 2 : (h + 1) * P // 2, :].rearrange("p t m j -> p m j t"),
                     raw[h][:].rearrange("p j (m t) -> p m j t", t=PACK),
                 )
-            banks = []
-            for t in range(PACK):
-                codes = keep.tile([P, P], U32, name=f"{name}_codes{t}", align_bytes=64)
-                plane = keep.tile([P, P], U8, name=f"{name}_plane{t}", align_bytes=64)
-                nc.vector.quantize_mx(
-                    out=codes[:].bitcast(FP8X4),
-                    scales=plane[:],
-                    in_=grouped[:, t, :, :].rearrange("p m j -> p (m j)"),
-                )
-                bank = psum.tile([P, S], F32, name=f"{name}_bank{t}")
-                nc.tensor.matmul_mx(
-                    out=bank[:],
-                    lhsT=codes[:].bitcast(FP8X4),
-                    lhsT_scale=plane[:],
-                    rhs=x_codes[:].bitcast(FP8X4),
-                    rhs_scale=x_plane[:],
-                    start=True,
-                    stop=True,
-                )
-                banks.append(bank)
-            return banks
+            return grouped
 
-        score_banks = first_product(w2_raw, "w2", nc.scalar.copy)
-        half_tanhs = []
-        for t in range(PACK):
+        def times_tokens(grouped, t, name, codes_tag):
+            codes = keep.tile([P, P], U32, name=f"{name}_codes", tag=codes_tag, align_bytes=64)
+            plane = keep.tile([P, P], U8, name=f"{name}_plane", align_bytes=64)
+            nc.vector.quantize_mx(
+                out=codes[:].bitcast(FP8X4),
+                scales=plane[:],
+                in_=grouped[:, t, :, :].rearrange("p m j -> p (m j)"),
+            )
+            bank = psum.tile([P, S], F32, name=name)
+            nc.tensor.matmul_mx(
+                out=bank[:],
+                lhsT=codes[:].bitcast(FP8X4),
+                lhsT_scale=plane[:],
+                rhs=x_codes[:].bitcast(FP8X4),
+                rhs_scale=x_plane[:],
+                start=True,
+                stop=True,
+            )
+            return bank
+
+        def score(t, codes_tag):
+            bank = times_tokens(w2_grouped, t, f"w2_bank{t}", codes_tag)
             half_tanh = keep.tile([P, S], F32, name=f"half_tanh{t}")
-            nc.scalar.activation(half_tanh[:], score_banks[t][:], ACT.Tanh, scale=0.5)
-            half_tanhs.append(half_tanh)
+            nc.scalar.activation(half_tanh[:], bank[:], ACT.Tanh, scale=0.5)
+            return half_tanh
 
-        value_banks = first_product(w1_raw, "w1", nc.vector.tensor_copy)
-        merged, pres = [], []
-        for t in range(PACK):
+        def value(t):
+            bank = times_tokens(w1_grouped, t, f"w1_bank{t}", f"w1_codes{t}")
             y = keep.tile([P, S], F32, name=f"merged{t}")
             copy = nc.vector.tensor_copy if t == 0 else nc.scalar.copy
-            copy(y[:], value_banks[t][:])
+            copy(y[:], bank[:])
             pre = keep.tile([P, V], F32, name=f"pre{t}")
             nc.vector.tensor_tensor(pre[:], y[:].indirect(sel_sb[:]), ctx_sb[:, t, :], ALU.add)
-            merged.append(y)
-            pres.append(pre)
+            return y, pre
+
+        w2_grouped = group_weight(w2_raw, "w2", nc.scalar.copy)
+        half_tanhs = [score(t, f"w2_codes{t}") for t in range(PACK - 1)]
+        w1_grouped = group_weight(w1_raw, "w1", nc.vector.tensor_copy)
+        values = [value(t) for t in range(PACK)]
+        half_tanhs.append(score(PACK - 1, "w1_raw1"))
+        merged = [y for y, pre in values]
+        pres = [pre for y, pre in values]
 
         w3_grouped = keep.tile([P, N, PACK], BF16, name="w3_grouped", align_bytes=64)
         nc.vector.tensor_copy(
@@ -156,37 +163,45 @@ def tile_picked_ymodsk_gain_p_kernel(
                 nc.vector.tensor_tensor(upd[:], gates[t], silus[t][:], ALU.mult)
                 nc.scalar.activation(window, upd[:], ACT.Copy)
 
-        hid = [keep.tile([P, PACK, HALF], BF16, name=f"hid{h}") for h in range(2)]
-        for t in (0, 3, 1, 2):
-            for h in (1, 0):
-                cols = slice(h * HALF, (h + 1) * HALF)
-                nc.vector.scalar_tensor_tensor(
-                    hid[h][:, t, :],
-                    merged[t][:, cols],
-                    unit_sb[:, t : t + 1],
-                    gn_sb[:, t, cols],
-                    ALU.mult,
-                    ALU.mult,
-                )
+        hid = keep.tile([P, PACK, S], BF16, name="hid")
 
-        copies = (nc.vector.tensor_copy, nc.scalar.copy)
-        for h in range(2):
-            cols = slice(h * HALF, (h + 1) * HALF)
-            grouped = keep.tile([P, HALF, PACK], BF16, name=f"hid_grouped{h}", align_bytes=64)
-            copies[h](
-                grouped[:].rearrange("p (c i) t -> p c t i", i=4),
-                hid[h][:].rearrange("p t (c i) -> p c t i", i=4),
+        def scale(t, cols):
+            nc.vector.scalar_tensor_tensor(
+                hid[:, t, cols],
+                merged[t][:, cols],
+                unit_sb[:, t : t + 1],
+                gn_sb[:, t, cols],
+                ALU.mult,
+                ALU.mult,
             )
-            codes = keep.tile([P, HALF], U32, name=f"hid_codes{h}", align_bytes=64)
-            plane = keep.tile([P, HALF], U8, name=f"hid_plane{h}", align_bytes=64)
+
+        quarters = [slice(c * P, (c + 1) * P) for c in range(S // P)]
+        for t in (0, 3, 1):
+            scale(t, slice(0, S))
+        for c in (1, 3, 0, 2):
+            scale(2, quarters[c])
+
+        hid_grouped = []
+        for c, cols in enumerate(quarters):
+            grouped = keep.tile([P, P, PACK], BF16, name=f"hid_grouped{c}", align_bytes=64)
+            copy = nc.scalar.copy if c % 2 else nc.vector.tensor_copy
+            copy(
+                grouped[:].rearrange("p (c i) t -> p c t i", i=4),
+                hid[:, :, cols].rearrange("p t (c i) -> p c t i", i=4),
+            )
+            hid_grouped.append(grouped)
+
+        for c in (1, 0, 2, 3):
+            codes = keep.tile([P, P], U32, name=f"hid_codes{c}", align_bytes=64)
+            plane = keep.tile([P, P], U8, name=f"hid_plane{c}", align_bytes=64)
             nc.vector.quantize_mx(
                 out=codes[:].bitcast(FP8X4),
                 scales=plane[:],
-                in_=grouped[:].rearrange("p c t -> p (c t)"),
+                in_=hid_grouped[c][:].rearrange("p c t -> p (c t)"),
             )
-            bank = psum.tile([P, S], F32, name=f"w2_bank{h}")
+            bank = psum.tile([P, S], F32, name=f"w2_bank{c}")
             nc.tensor.matmul_mx(
-                out=bank[:, 0:HALF],
+                out=bank[:, 0:P],
                 lhsT=w3_codes[:].bitcast(FP8X4),
                 lhsT_scale=w3_plane[:],
                 rhs=codes[:].bitcast(FP8X4),
@@ -194,6 +209,7 @@ def tile_picked_ymodsk_gain_p_kernel(
                 start=True,
                 stop=True,
             )
-            result = keep.tile([P, HALF], F32, name=f"result{h}")
-            copies[1 - h](result[:], bank[:, 0:HALF])
-            nc.sync.dma_start(out[:, cols], result[:])
+            result = keep.tile([P, P], F32, name=f"result{c}")
+            copy = nc.vector.tensor_copy if c == 3 else nc.scalar.copy
+            copy(result[:], bank[:, 0:P])
+            nc.sync.dma_start(out[:, quarters[c]], result[:])

from contextlib import ExitStack

import concourse.mybir as mybir

K, T, S, N, H, V = 512, 1024, 512, 128, 512, 256
FLOPS = 2 * K * H * S * 2 + 2 * H * N * S

F32 = mybir.dt.float32
BF16 = mybir.dt.bfloat16
I32 = mybir.dt.int32
U32 = mybir.dt.uint32
U16 = mybir.dt.uint16
U8 = mybir.dt.uint8
FP8X4 = mybir.dt.float8_e4m3fn_x4
ACT = mybir.ActivationFunctionType
ALU = mybir.AluOpType

P = 128
PACK = 4
HALF = H // 2
SCATTER_ON_VECTOR = (0, 3)


def tile_picked_ymodsk_gain_p_kernel(
    tc, x_words, x_scales, w1, w2, ctx2, gn, unit, w3, offs, sel, out
):
    nc = tc.nc
    with ExitStack() as ctx:
        keep = ctx.enter_context(tc.tile_pool(name="keep", bufs=1))
        psum = ctx.enter_context(tc.psum_pool(name="psum", bufs=1))

        offs_sb = keep.tile([P, S // 16], U16, name="offs_sb")
        sel_sb = keep.tile([P, V // 16], U16, name="sel_sb")
        table_words = keep.tile([P, T], U32, name="table_words", align_bytes=64)
        table_bytes = keep.tile([P, T], U8, name="table_bytes", align_bytes=64)

        nc.vector.memset(table_bytes[:].bitcast(I32), 0)
        warm = keep.tile([P, 2], F32, name="warm")
        nc.gpsimd.memset(warm[:, 0:1], 0.0)
        nc.scalar.activation(warm[:, 1:2], warm[:, 0:1], ACT.Silu)
        nc.sync.dma_start(offs_sb[:], offs)
        nc.sync.dma_start(
            table_words[:].bitcast(I32), x_words[0].rearrange("p c r -> p (c r)").bitcast(I32)
        )
        for q in range(4):
            nc.sync.dma_start(
                table_bytes[32 * q : 32 * q + 4, :].bitcast(I32),
                x_scales[0, 4 * q : 4 * q + 4, :].bitcast(I32),
            )

        def load_halves(w, name):
            halves = []
            for h in range(2):
                raw = keep.tile([P, PACK, HALF], F32, name=f"{name}_raw{h}", align_bytes=64)
                nc.sync.dma_start(
                    raw[:], w.rearrange("(p j) c -> p j c", j=PACK)[:, :, h * HALF : (h + 1) * HALF]
                )
                halves.append(raw)
            return halves

        w2_raw = load_halves(w2, "w2")
        w1_raw = load_halves(w1, "w1")
        nc.sync.dma_start(sel_sb[:], sel)
        ctx_sb = keep.tile([P, PACK, V], F32, name="ctx_sb")
        nc.sync.dma_start(ctx_sb[:], ctx2.rearrange("(p t) v -> p t v", t=PACK))
        w3_raw = keep.tile([P, PACK, N], F32, name="w3_raw")
        nc.sync.dma_start(w3_raw[:], w3.rearrange("(p j) c -> p j c", j=PACK))
        unit_sb = keep.tile([P, PACK], F32, name="unit_sb")
        nc.sync.dma_start(unit_sb[:], unit.rearrange("(p t) o -> p (t o)", t=PACK))
        gn_sb = keep.tile([P, PACK, S], F32, name="gn_sb")
        nc.sync.dma_start(gn_sb[:], gn.rearrange("(p t) c -> p t c", t=PACK))

        x_codes = keep.tile([P, S], U32, name="x_codes", align_bytes=64)
        x_plane = keep.tile([P, S], U8, name="x_plane", align_bytes=64)
        nc.vector.tensor_copy(x_codes[:], table_words[:].indirect(offs_sb[:]))
        nc.vector.tensor_copy(x_plane[:], table_bytes[:].indirect(offs_sb[:]))

        def group_weight(raw, name, first_half_copy):
            grouped = keep.tile(
                [P, PACK, P, PACK], BF16, name=f"{name}_grouped", tag=f"{name}_stage", align_bytes=64
            )
            for h, copy in enumerate((first_half_copy, nc.vector.tensor_copy)):
                copy(
                    grouped[:, :, h * P // 2 : (h + 1) * P // 2, :].rearrange("p t m j -> p m j t"),
                    raw[h][:].rearrange("p j (m t) -> p m j t", t=PACK),
                )
            return grouped

        def times_tokens(grouped, t, name, codes_tag):
            codes = keep.tile([P, P], U32, name=f"{name}_codes", tag=codes_tag, align_bytes=64)
            plane = keep.tile([P, P], U8, name=f"{name}_plane", align_bytes=64)
            nc.vector.quantize_mx(
                out=codes[:].bitcast(FP8X4),
                scales=plane[:],
                in_=grouped[:, t, :, :].rearrange("p m j -> p (m j)"),
            )
            bank = psum.tile([P, S], F32, name=name)
            nc.tensor.matmul_mx(
                out=bank[:],
                lhsT=codes[:].bitcast(FP8X4),
                lhsT_scale=plane[:],
                rhs=x_codes[:].bitcast(FP8X4),
                rhs_scale=x_plane[:],
                start=True,
                stop=True,
            )
            return bank

        def score(t, codes_tag):
            bank = times_tokens(w2_grouped, t, f"w2_bank{t}", codes_tag)
            half_tanh = keep.tile([P, S], F32, name=f"half_tanh{t}")
            nc.scalar.activation(half_tanh[:], bank[:], ACT.Tanh, scale=0.5)
            return half_tanh

        def value(t):
            bank = times_tokens(w1_grouped, t, f"w1_bank{t}", f"w1_codes{t}")
            y = keep.tile([P, S], F32, name=f"merged{t}")
            copy = nc.vector.tensor_copy if t == 0 else nc.scalar.copy
            copy(y[:], bank[:])
            pre = keep.tile([P, V], F32, name=f"pre{t}")
            nc.vector.tensor_tensor(pre[:], y[:].indirect(sel_sb[:]), ctx_sb[:, t, :], ALU.add)
            return y, pre

        w2_grouped = group_weight(w2_raw, "w2", nc.scalar.copy)
        half_tanhs = [score(t, f"w2_codes{t}") for t in range(PACK - 1)]
        w1_grouped = group_weight(w1_raw, "w1", nc.vector.tensor_copy)
        values = [value(t) for t in range(PACK)]
        half_tanhs.append(score(PACK - 1, "w1_raw1"))
        merged = [y for y, pre in values]
        pres = [pre for y, pre in values]

        w3_grouped = keep.tile([P, N, PACK], BF16, name="w3_grouped", align_bytes=64)
        nc.vector.tensor_copy(
            w3_grouped[:].rearrange("p (c i) j -> p c j i", i=4),
            w3_raw[:].rearrange("p j (c i) -> p c j i", i=4),
        )
        w3_codes = keep.tile([P, N], U32, name="w3_codes", align_bytes=64)
        w3_plane = keep.tile([P, N], U8, name="w3_plane", align_bytes=64)
        nc.vector.quantize_mx(
            out=w3_codes[:].bitcast(FP8X4),
            scales=w3_plane[:],
            in_=w3_grouped[:].rearrange("p c j -> p (c j)"),
        )

        gates, silus = [], []
        gate_tile = keep.tile([P, PACK, V], F32, name="gate_tile", tag="w1_stage", align_bytes=64)
        for t in range(PACK):
            silu = keep.tile([P, V], F32, name=f"silu{t}")
            nc.scalar.activation(silu[:], pres[t][:], ACT.Silu)
            gate = gate_tile[:, t, :]
            nc.scalar.activation(
                gate, half_tanhs[t][:].indirect(sel_sb[:]), ACT.Copy, scale=0.5, bias=0.5
            )
            gates.append(gate)
            silus.append(silu)

        for t in range(PACK):
            window = merged[t][:].indirect(sel_sb[:])
            if t in SCATTER_ON_VECTOR:
                nc.vector.tensor_tensor(window, gates[t], silus[t][:], ALU.mult)
            else:
                upd = keep.tile([P, V], F32, name=f"upd{t}")
                nc.vector.tensor_tensor(upd[:], gates[t], silus[t][:], ALU.mult)
                nc.scalar.activation(window, upd[:], ACT.Copy)

        hid = keep.tile([P, PACK, S], BF16, name="hid")

        def scale(t, cols):
            nc.vector.scalar_tensor_tensor(
                hid[:, t, cols],
                merged[t][:, cols],
                unit_sb[:, t : t + 1],
                gn_sb[:, t, cols],
                ALU.mult,
                ALU.mult,
            )

        quarters = [slice(c * P, (c + 1) * P) for c in range(S // P)]
        for t in (0, 3, 1):
            scale(t, slice(0, S))
        for c in (1, 3, 0, 2):
            scale(2, quarters[c])

        hid_grouped = []
        for c, cols in enumerate(quarters):
            grouped = keep.tile([P, P, PACK], BF16, name=f"hid_grouped{c}", align_bytes=64)
            copy = nc.scalar.copy if c % 2 else nc.vector.tensor_copy
            copy(
                grouped[:].rearrange("p (c i) t -> p c t i", i=4),
                hid[:, :, cols].rearrange("p t (c i) -> p c t i", i=4),
            )
            hid_grouped.append(grouped)

        for c in (1, 0, 2, 3):
            codes = keep.tile([P, P], U32, name=f"hid_codes{c}", align_bytes=64)
            plane = keep.tile([P, P], U8, name=f"hid_plane{c}", align_bytes=64)
            nc.vector.quantize_mx(
                out=codes[:].bitcast(FP8X4),
                scales=plane[:],
                in_=hid_grouped[c][:].rearrange("p c t -> p (c t)"),
            )
            bank = psum.tile([P, S], F32, name=f"w2_bank{c}")
            nc.tensor.matmul_mx(
                out=bank[:, 0:P],
                lhsT=w3_codes[:].bitcast(FP8X4),
                lhsT_scale=w3_plane[:],
                rhs=codes[:].bitcast(FP8X4),
                rhs_scale=plane[:],
                start=True,
                stop=True,
            )
            result = keep.tile([P, P], F32, name=f"result{c}")
            copy = nc.vector.tensor_copy if c == 3 else nc.scalar.copy
            copy(result[:], bank[:, 0:P])
            nc.sync.dma_start(out[:, quarters[c]], result[:])
